import numpy as np
import ml_dtypes


def mxq(x, axis, fmt="e4m3"):
    dtype, down = {"e4m3": (ml_dtypes.float8_e4m3fn, 7), "e5m2": (ml_dtypes.float8_e5m2, 14)}[fmt]
    v = np.moveaxis(np.asarray(x, np.float32).astype(ml_dtypes.bfloat16).astype(np.float64), axis, -1)
    blocks = v.reshape(v.shape[:-1] + (-1, 32))
    amax = np.abs(blocks).max(-1, keepdims=True)
    byte = np.maximum(np.where(amax > 0, np.frexp(amax)[1] - 1 + 127, 0) - down, 1)
    scale = np.exp2(byte - 127.0)
    codes = (blocks / scale).astype(np.float32).astype(dtype).astype(np.float64)
    return np.moveaxis((codes * scale).reshape(v.shape), -1, axis)


WIDE = False


def mx_kscale(k):
    if not WIDE:
        return np.ones(k)
    levels = np.array([10, -10, 5, -5, 0])
    if k % 512:
        return np.exp2(np.random.permutation(np.resize(levels, k // 32))).repeat(32)
    a = np.empty((k // 512, 16))
    for p in range(k // 512):
        a[p, :8] = np.random.permutation(np.resize(levels, 8))
        for g in range(8):
            far = levels[np.abs(levels - a[p, g]) >= 10]
            a[p, g + 8] = far[np.random.randint(len(far))]
    return np.exp2(a.ravel()).repeat(32)


def f64(x):
    return np.asarray(x).astype(np.float64)


def striped(idx):
    return np.tile(idx.reshape(-1, 16).T, (8, 1)).astype(np.uint16)


def unstriped(offs):
    return offs[:16].T.reshape(-1).astype(np.int64)


def pack_weight(w):
    k, n = w.shape
    w = f64(np.asarray(w, np.float32).astype(ml_dtypes.bfloat16)).reshape(k // 32, 32, n)
    amax = np.abs(w).max(1)
    byte = np.clip(np.where(amax > 0, np.frexp(amax)[1] - 1 + 127 - 7, 1), 1, 254)
    scaled = (w * np.exp2(127.0 - byte)[:, None, :]).reshape(k, n).astype(np.float32)
    words = np.ascontiguousarray(scaled.reshape(k // 512, 128, 4, n).transpose(0, 1, 3, 2)).astype(ml_dtypes.float8_e4m3fn).view(np.uint8)
    return words, np.ascontiguousarray(byte.astype(np.uint8).reshape(k // 512, 16, n))


def unpack_weight(words, scales):
    g, p, n, _ = words.shape
    vals = np.ascontiguousarray(words).view(ml_dtypes.float8_e4m3fn).astype(np.float64) * np.repeat(np.exp2(scales.astype(np.float64) - 127.0), 8, axis=1)[..., None]
    return vals.transpose(0, 1, 3, 2).reshape(g * 512, n)


def planes(y):
    n, m = y.shape
    v = y.astype(np.float32).astype(ml_dtypes.bfloat16).astype(np.float64).reshape(n // 32, 32, m)
    top = np.abs(v).max(1)
    byte = np.clip(np.where(top > 0, np.frexp(top)[1] - 1 + 127 - 7, 1), 1, 254)
    codes = (v * np.exp2(127.0 - byte)[:, None, :]).reshape(n, m).astype(np.float32).astype(ml_dtypes.float8_e4m3fn).view(np.uint8)
    words = codes.reshape(n // 512, 128, 4, m).transpose(0, 1, 3, 2)
    return np.ascontiguousarray(words), np.ascontiguousarray(byte.astype(np.uint8).reshape(n // 512, 16, m))


def relu(v):
    return np.maximum(v, 0.0)


K, T, S, D, V, H, N = 512, 2048, 512, 3, 256, 512, 512
P = 2 ** 7


def setup_inputs():
    n = np.random.standard_normal
    s = mx_kscale(K)[:, None]
    u = mx_kscale(H)
    near = np.random.permutation(S)
    packed_xT = pack_weight(n((K, T)) * s)
    return {
        "x_words": packed_xT[0],
        "x_scales": packed_xT[1],
        "w1": (n((K, H)) / np.sqrt(K) / s * u).astype(np.float32),
        "w2": (n((H, N)) / np.sqrt(2 * H) / u[:, None]).astype(np.float32),
        "gate": (np.tile(np.random.uniform(0.2, 1.0, (D, 1, V)) / np.sqrt(D), (1, P, 1))).astype(np.float32),
        "eT": (n((K, V)) * s).astype(np.float32),
        "w3": (n((K, N)) / np.sqrt(2 * K) / s).astype(np.float32),
        "offs": striped(np.random.permutation(T)[:S]),
        "pos1": striped(near[:V]),
        "pos2": striped(near[V:]),
        "pos3": striped(np.random.permutation(S)[:V]),
    }


def reference(x_words, x_scales, w1, w2, gate, eT, w3, offs, pos1, pos2, pos3):
    xq = unpack_weight(x_words, x_scales)[:, unstriped(offs)]
    h = relu(mxq(f64(w1), 0, "e4m3").T @ xq)
    z = h[:, unstriped(pos1)] * f64(gate)[0, :1] + h[:, unstriped(pos2)] * f64(gate)[1, :1] + h[:, unstriped(pos3)] * f64(gate)[2, :1]
    eTq = mxq(f64(eT), 0, "e4m3")
    out_0 = relu(mxq(f64(w2), 0, "e4m3").T @ mxq(z, 0, "e4m3") + mxq(f64(w3), 0, "e4m3").T @ eTq)
    return (out_0,) + planes(out_0)

@@ -1,0 +1,258 @@
+from contextlib import ExitStack
+
+import concourse.mybir as mybir
+from concourse.masks import make_identity
+
+K, T, S, D, V, H, N = 512, 2048, 512, 3, 256, 512, 512
+FLOPS = 2 * (K * H * S + H * N * V + K * N * V)
+
+F32 = mybir.dt.float32
+BF16 = mybir.dt.bfloat16
+I32 = mybir.dt.int32
+U32 = mybir.dt.uint32
+U16 = mybir.dt.uint16
+U8 = mybir.dt.uint8
+FP8X4 = mybir.dt.float8_e4m3fn_x4
+MULT = mybir.AluOpType.mult
+COPY = mybir.ActivationFunctionType.Copy
+RELU = mybir.ActivationFunctionType.Relu
+
+P = 128
+PACK = 4
+HALF = V // 2
+QUADS = 4
+W1_SPLIT = 48
+
+
+def tile_picked_zfp_relu_po_kernel(
+    tc, x_words, x_scales, w1, w2, gate, eT, w3, offs, pos1, pos2, pos3, out_0, out_1, out_2
+):
+    nc = tc.nc
+    with ExitStack() as ctx:
+        lists = ctx.enter_context(tc.tile_pool(name="lists", bufs=1))
+        keep = ctx.enter_context(tc.tile_pool(name="keep", bufs=1))
+        psum = ctx.enter_context(tc.psum_pool(name="psum", bufs=1))
+
+        def sb(name, shape, dtype, tag=None):
+            return keep.tile(shape, dtype, name=name, tag=tag or name, align_bytes=64)
+
+        def bank(number, name):
+            return psum.tile([P, 512], F32, name=name, tag="bank%d" % number)
+
+        def load_rows(name, src):
+            raw = sb(name, [P, PACK, src.shape[1]], F32)
+            nc.sync.dma_start(out=raw[:], in_=src.rearrange("(p j) c -> p j c", j=PACK))
+            return raw
+
+        def round_on(engine, out, in_):
+            if engine == "vector":
+                nc.vector.tensor_copy(out=out, in_=in_)
+            else:
+                nc.scalar.activation(out=out, in_=in_, func=COPY)
+
+        def relu_on(engine, out, in_):
+            if engine == "vector":
+                nc.vector.tensor_scalar_max(out=out, in0=in_, scalar1=0.0)
+            else:
+                nc.scalar.activation(out=out, in_=in_, func=RELU)
+
+        def deal(engine, grouped, raw, m0, m1):
+            round_on(
+                engine,
+                grouped[:].rearrange("p (t m j) -> p m j t", t=PACK, j=PACK)[:, m0:m1],
+                raw[:].rearrange("p j (m t) -> p m j t", t=PACK)[:, m0:m1],
+            )
+
+        def interleave(engine, grouped, raw):
+            round_on(
+                engine,
+                grouped[:].rearrange("p (c i j) -> p c j i", i=4, j=PACK),
+                raw[:].rearrange("p j (c i) -> p c j i", i=4),
+            )
+
+        def quantize(codes, scales, grouped):
+            nc.vector.quantize_mx(out=codes.bitcast(FP8X4), scales=scales, in_=grouped)
+
+        def mx(out, a, cols_a, b, cols_b, start, stop):
+            nc.tensor.matmul_mx(
+                out=out,
+                lhsT=a[0][:, cols_a].bitcast(FP8X4),
+                lhsT_scale=a[1][:, cols_a],
+                rhs=b[0][:, cols_b].bitcast(FP8X4),
+                rhs_scale=b[1][:, cols_b],
+                start=start,
+                stop=stop,
+            )
+
+        def operand(name, width):
+            return sb(name + "_codes", [P, width], U32), sb(name + "_scales", [P, width], U8)
+
+        def block(i, width=P):
+            return slice(i * width, (i + 1) * width)
+
+        offs_sb = lists.tile([P, S // 16], U16, name="offs_sb")
+        nc.sync.dma_start(offs_sb[:], offs)
+        w1_raw = load_rows("w1_raw", w1)
+
+        xs_all = sb("xs_all", [P, T], U8)
+        nc.gpsimd.memset(xs_all[:].bitcast(I32), 0)
+        for q in range(QUADS):
+            nc.sync.dma_start(
+                out=xs_all[32 * q : 32 * q + 4, :].bitcast(I32),
+                in_=x_scales[0, 4 * q : 4 * q + 4, :].bitcast(I32),
+            )
+        xw_all = sb("xw_all", [P, T], I32)
+        nc.sync.dma_start(out=xw_all[:], in_=x_words[0].rearrange("p c r -> p (c r)").bitcast(I32))
+
+        e_raw = load_rows("e_raw", eT)
+        pos_sb = []
+        for d, pos in enumerate((pos1, pos2, pos3)):
+            one = lists.tile([P, V // 16], U16, name="pos%d_sb" % d)
+            nc.sync.dma_start(one[:], pos)
+            pos_sb.append(one)
+        gate_sb = sb("gate_sb", [P, D, V], F32)
+        nc.sync.dma_start(out=gate_sb[:], in_=gate.rearrange("d p v -> p d v"))
+        w3_raw = load_rows("w3_raw", w3)
+        w2_raw = load_rows("w2_raw", w2)
+
+        ident = sb("ident", [P, P], F32)
+        make_identity(nc, ident[:])
+
+        xq = operand("x", S)
+        nc.vector.tensor_copy(out=xq[1][:], in_=xs_all[:].indirect(offs_sb[:]))
+
+        w1_g = sb("w1_g", [P, PACK * H], BF16)
+        deal("vector", w1_g, w1_raw, 0, W1_SPLIT)
+        deal("scalar", w1_g, w1_raw, W1_SPLIT, P)
+        w1q = operand("w1", H)
+        quantize(w1q[0][:], w1q[1][:], w1_g[:])
+
+        for a in range(2):
+            nc.vector.tensor_copy(
+                out=xq[0][:, block(a, S // 2)],
+                in_=xw_all[:].bitcast(U32).indirect(offs_sb[:, block(a, S // 32)]),
+            )
+
+        e_g = sb("e_g", [P, PACK * V], BF16)
+        interleave("vector", e_g, e_raw)
+        eq = operand("e", V)
+        quantize(eq[0][:], eq[1][:], e_g[:])
+
+        h = [sb("h%d" % t, [P, S], F32) for t in range(PACK)]
+        h0a, h0b, h1, h2, h3 = [bank(i, "hbank%d" % i) for i in range(5)]
+        first, second = block(0, S // 2), block(1, S // 2)
+        mx(h0a[:, first], w1q, block(0), xq, first, True, True)
+        mx(h1[:, first], w1q, block(1), xq, first, True, True)
+        mx(h0b[:, first], w1q, block(0), xq, second, True, True)
+        mx(h1[:, second], w1q, block(1), xq, second, True, True)
+        mx(h2[:], w1q, block(2), xq, slice(0, S), True, True)
+        mx(h3[:], w1q, block(3), xq, slice(0, S), True, True)
+        relu_on("scalar", h[0][:, first], h0a[:, first])
+        relu_on("scalar", h[0][:, second], h0b[:, first])
+        for t, src in ((1, h1), (2, h2), (3, h3)):
+            relu_on("scalar", h[t][:], src[:])
+
+        prod = [[sb("prod%d_%d" % (t, d), [P, V], F32) for d in range(D)] for t in range(PACK - 1)]
+
+        def gather(t, d, a0, a1):
+            cols = slice(a0 * HALF, a1 * HALF)
+            nc.vector.tensor_tensor(
+                out=prod[t][d][:, cols],
+                in0=h[t][:].indirect(pos_sb[d][:, a0 * HALF // 16 : a1 * HALF // 16]),
+                in1=gate_sb[:, d, cols],
+                op=MULT,
+            )
+
+        def add_turned(out, t, a):
+            for d in range(D):
+                nc.tensor.matmul(
+                    out, lhsT=prod[t][d][:, block(a)], rhs=ident[:], is_transpose=True, start=(d == 0), stop=(d == D - 1)
+                )
+
+        zt_low = bank(5, "zt_low")
+        zt_high = [bank(6, "zt_high0"), bank(7, "zt_high1")]
+
+        for t in range(2):
+            for d in range(D):
+                gather(t, d, 0, 2)
+            for a in range(2):
+                add_turned(zt_low[:, block(2 * a + t)], t, a)
+
+        w3_g = sb("w3_g", [P, PACK * N], BF16)
+        deal("scalar", w3_g, w3_raw, 0, P // 2)
+        deal("scalar", w3_g, w3_raw, P // 2, P)
+
+        pairs_low = sb("pairs_low", [P, 2 * V], BF16, tag="w3_raw")
+        nc.scalar.activation(
+            out=pairs_low[:].rearrange("v (a p e) -> v a p e", a=2, e=2),
+            in_=zt_low[:].rearrange("v (a e p) -> v a p e", a=2, e=2),
+            func=COPY,
+        )
+        back = [bank(0, "back0"), bank(1, "back1")]
+        for a in range(2):
+            nc.tensor.transpose(back[a][:, block(0)], pairs_low[:].bitcast(F32)[:, block(a)], ident[:])
+
+        for d in range(D):
+            gather(2, d, 0, 2)
+        for a in range(2):
+            add_turned(zt_high[a][:, block(0)], 2, a)
+
+        w3q = operand("w3", N)
+        quantize(w3q[0][:], w3q[1][:], w3_g[:])
+
+        acc = [[bank(2, "acc00"), bank(5, "acc01")], [bank(3, "acc10"), bank(4, "acc11")]]
+        for a in range(2):
+            for t in range(PACK):
+                mx(acc[a][t // 2][:, block(t % 2)], w3q, block(t), eq, block(a), t % 2 == 0, False)
+
+        w2_g = sb("w2_g", [P, PACK * N], BF16)
+        deal("scalar", w2_g, w2_raw, 0, P // 2)
+        deal("scalar", w2_g, w2_raw, P // 2, P)
+        last = sb("prod3", [P, D, V], F32, tag="w3_g")
+        prod.append([last[:, d, :] for d in range(D)])
+        for a in range(2):
+            for d in range(D):
+                gather(3, d, a, a + 1)
+            add_turned(zt_high[a][:, block(1)], 3, a)
+        w2q = operand("w2", N)
+        quantize(w2q[0][:], w2q[1][:], w2_g[:])
+
+        oq = operand("out", V)
+        out_rows = out_0.rearrange("(p t) v -> p t v", t=PACK)
+        out_words = out_1[0].rearrange("p c r -> p (c r)").bitcast(I32)
+        pairs_high = sb("pairs_high", [P, 2 * V], BF16, tag="w2_raw")
+        for a in range(2):
+            helper = ("scalar", "vector")[a]
+            round_on(
+                "scalar",
+                pairs_high[:, block(a, V)].rearrange("v (p e) -> v p e", e=2),
+                zt_high[a][:, 0:V].rearrange("v (e p) -> v p e", e=2),
+            )
+            nc.tensor.transpose(back[a][:, block(1)], pairs_high[:].bitcast(F32)[:, block(a)], ident[:])
+            z_g = sb("z_g%d" % a, [P, PACK * HALF], BF16)
+            nc.scalar.copy(
+                out=z_g[:].bitcast(F32).rearrange("p (v u) -> p v u", u=2),
+                in_=back[a][:, 0:V].rearrange("p (u v) -> p v u", u=2),
+            )
+            zq = operand("z%d" % a, HALF)
+            quantize(zq[0][:], zq[1][:], z_g[:])
+            for t in range(PACK):
+                mx(acc[a][t // 2][:, block(t % 2)], w2q, block(t), zq, slice(0, HALF), False, t % 2 == 1)
+            y = sb("y%d" % a, [P, PACK, HALF], F32)
+            for pair, engine in enumerate(("scalar", helper)):
+                relu_on(
+                    engine,
+                    y[:, 2 * pair : 2 * pair + 2, :],
+                    acc[a][pair][:, 0:V].rearrange("p (t v) -> p t v", t=2),
+                )
+            nc.sync.dma_start(out=out_rows[:, :, block(a)], in_=y[:])
+            y_g = sb("y_g%d" % a, [P, PACK * HALF], BF16)
+            interleave("vector", y_g, y)
+            quantize(oq[0][:, block(a)], oq[1][:, block(a)], y_g[:])
+            nc.sync.dma_start(out=out_words[:, block(a)], in_=oq[0][:, block(a)].bitcast(I32))
+        for q in range(QUADS):
+            queue = nc.scalar if q % 2 else nc.sync
+            queue.dma_start(
+                out=out_2[0, 4 * q : 4 * q + 4, :].bitcast(I32),
+                in_=oq[1][32 * q : 32 * q + 4, :].bitcast(I32),
+            )

@@ -21,7 +21,6 @@ P = 128
 PACK = 4
 HALF = V // 2
 QUADS = 4
-W1_SPLIT = 48
 
 
 def tile_picked_zfp_relu_po_kernel(
@@ -39,9 +38,9 @@ def tile_picked_zfp_relu_po_kernel(
         def bank(number, name):
             return psum.tile([P, 512], F32, name=name, tag="bank%d" % number)
 
-        def load_rows(name, src):
-            raw = sb(name, [P, PACK, src.shape[1]], F32)
-            nc.sync.dma_start(out=raw[:], in_=src.rearrange("(p j) c -> p j c", j=PACK))
+        def load_rows(name, src, cols):
+            raw = sb(name, [P, PACK, cols.stop - cols.start], F32)
+            nc.sync.dma_start(out=raw[:], in_=src.rearrange("(p j) c -> p j c", j=PACK)[:, :, cols])
             return raw
 
         def round_on(engine, out, in_):
@@ -92,7 +91,7 @@ def tile_picked_zfp_relu_po_kernel(
 
         offs_sb = lists.tile([P, S // 16], U16, name="offs_sb")
         nc.sync.dma_start(offs_sb[:], offs)
-        w1_raw = load_rows("w1_raw", w1)
+        w1_raw = [load_rows("w1_raw0", w1, block(0, H // 2))]
 
         xs_all = sb("xs_all", [P, T], U8)
         nc.gpsimd.memset(xs_all[:].bitcast(I32), 0)
@@ -104,7 +103,7 @@ def tile_picked_zfp_relu_po_kernel(
         xw_all = sb("xw_all", [P, T], I32)
         nc.sync.dma_start(out=xw_all[:], in_=x_words[0].rearrange("p c r -> p (c r)").bitcast(I32))
 
-        e_raw = load_rows("e_raw", eT)
+        w1_raw.append(load_rows("w1_raw1", w1, block(1, H // 2)))
         pos_sb = []
         for d, pos in enumerate((pos1, pos2, pos3)):
             one = lists.tile([P, V // 16], U16, name="pos%d_sb" % d)
@@ -112,8 +111,9 @@ def tile_picked_zfp_relu_po_kernel(
             pos_sb.append(one)
         gate_sb = sb("gate_sb", [P, D, V], F32)
         nc.sync.dma_start(out=gate_sb[:], in_=gate.rearrange("d p v -> p d v"))
-        w3_raw = load_rows("w3_raw", w3)
-        w2_raw = load_rows("w2_raw", w2)
+        e_raw = load_rows("e_raw", eT, slice(0, V))
+        w3_raw = load_rows("w3_raw", w3, slice(0, N))
+        w2_raw = load_rows("w2_raw", w2, slice(0, N))
 
         ident = sb("ident", [P, P], F32)
         make_identity(nc, ident[:])
@@ -121,38 +121,39 @@ def tile_picked_zfp_relu_po_kernel(
         xq = operand("x", S)
         nc.vector.tensor_copy(out=xq[1][:], in_=xs_all[:].indirect(offs_sb[:]))
 
-        w1_g = sb("w1_g", [P, PACK * H], BF16)
-        deal("vector", w1_g, w1_raw, 0, W1_SPLIT)
-        deal("scalar", w1_g, w1_raw, W1_SPLIT, P)
-        w1q = operand("w1", H)
-        quantize(w1q[0][:], w1q[1][:], w1_g[:])
+        w1_g = [sb("w1_g0", [P, PACK * H // 2], BF16), sb("w1_g1", [P, PACK * H // 2], BF16, tag="xw_all")]
+        w1q = [operand("w1_%d" % i, H // 2) for i in range(2)]
+        interleave("scalar", w1_g[0], w1_raw[0])
+        quantize(w1q[0][0][:], w1q[0][1][:], w1_g[0][:])
 
         for a in range(2):
             nc.vector.tensor_copy(
                 out=xq[0][:, block(a, S // 2)],
                 in_=xw_all[:].bitcast(U32).indirect(offs_sb[:, block(a, S // 32)]),
             )
-
-        e_g = sb("e_g", [P, PACK * V], BF16)
-        interleave("vector", e_g, e_raw)
-        eq = operand("e", V)
-        quantize(eq[0][:], eq[1][:], e_g[:])
+        interleave("vector", w1_g[1], w1_raw[1])
+        quantize(w1q[1][0][:], w1q[1][1][:], w1_g[1][:])
 
         h = [sb("h%d" % t, [P, S], F32) for t in range(PACK)]
         h0a, h0b, h1, h2, h3 = [bank(i, "hbank%d" % i) for i in range(5)]
         first, second = block(0, S // 2), block(1, S // 2)
-        mx(h0a[:, first], w1q, block(0), xq, first, True, True)
-        mx(h1[:, first], w1q, block(1), xq, first, True, True)
-        mx(h0b[:, first], w1q, block(0), xq, second, True, True)
-        mx(h1[:, second], w1q, block(1), xq, second, True, True)
-        mx(h2[:], w1q, block(2), xq, slice(0, S), True, True)
-        mx(h3[:], w1q, block(3), xq, slice(0, S), True, True)
+        mx(h0a[:, first], w1q[0], block(0), xq, first, True, True)
+        mx(h1[:, first], w1q[0], block(1), xq, first, True, True)
+        mx(h0b[:, first], w1q[0], block(0), xq, second, True, True)
+        mx(h1[:, second], w1q[0], block(1), xq, second, True, True)
+        mx(h2[:], w1q[1], block(0), xq, slice(0, S), True, True)
+        mx(h3[:], w1q[1], block(1), xq, slice(0, S), True, True)
         relu_on("scalar", h[0][:, first], h0a[:, first])
         relu_on("scalar", h[0][:, second], h0b[:, first])
         for t, src in ((1, h1), (2, h2), (3, h3)):
             relu_on("scalar", h[t][:], src[:])
 
-        prod = [[sb("prod%d_%d" % (t, d), [P, V], F32) for d in range(D)] for t in range(PACK - 1)]
+        reuse = ("xw_all", None, None, "e_raw")
+        prod = []
+
+        def new_products(t):
+            three = sb("prod%d" % t, [P, D, V], F32, tag=reuse[t])
+            prod.append([three[:, d, :] for d in range(D)])
 
         def gather(t, d, a0, a1):
             cols = slice(a0 * HALF, a1 * HALF)
@@ -169,66 +170,64 @@ def tile_picked_zfp_relu_po_kernel(
                     out, lhsT=prod[t][d][:, block(a)], rhs=ident[:], is_transpose=True, start=(d == 0), stop=(d == D - 1)
                 )
 
-        zt_low = bank(5, "zt_low")
-        zt_high = [bank(6, "zt_high0"), bank(7, "zt_high1")]
-
-        for t in range(2):
+        zt_early = [bank(5, "zt_early0"), bank(6, "zt_early1")]
+        zt_late = [bank(0, "zt_late0"), bank(1, "zt_late1")]
+        for t in range(PACK - 1):
+            new_products(t)
             for d in range(D):
                 gather(t, d, 0, 2)
             for a in range(2):
-                add_turned(zt_low[:, block(2 * a + t)], t, a)
+                add_turned(zt_early[a][:, block(t)], t, a)
 
-        w3_g = sb("w3_g", [P, PACK * N], BF16)
-        deal("scalar", w3_g, w3_raw, 0, P // 2)
-        deal("scalar", w3_g, w3_raw, P // 2, P)
+        e_g = sb("e_g", [P, PACK * V], BF16, tag="w1_1_codes")
+        interleave("scalar", e_g, e_raw)
+        eq = operand("e", V)
+        quantize(eq[0][:], eq[1][:], e_g[:])
 
-        pairs_low = sb("pairs_low", [P, 2 * V], BF16, tag="w3_raw")
-        nc.scalar.activation(
-            out=pairs_low[:].rearrange("v (a p e) -> v a p e", a=2, e=2),
-            in_=zt_low[:].rearrange("v (a e p) -> v a p e", a=2, e=2),
-            func=COPY,
-        )
-        back = [bank(0, "back0"), bank(1, "back1")]
-        for a in range(2):
-            nc.tensor.transpose(back[a][:, block(0)], pairs_low[:].bitcast(F32)[:, block(a)], ident[:])
-
-        for d in range(D):
-            gather(2, d, 0, 2)
-        for a in range(2):
-            add_turned(zt_high[a][:, block(0)], 2, a)
-
+        w3_g = sb("w3_g", [P, PACK * N], BF16, tag="e_raw")
+        deal("scalar", w3_g, w3_raw, 0, P)
         w3q = operand("w3", N)
         quantize(w3q[0][:], w3q[1][:], w3_g[:])
 
-        acc = [[bank(2, "acc00"), bank(5, "acc01")], [bank(3, "acc10"), bank(4, "acc11")]]
+        late_bf16 = sb("late_bf16", [P, PACK * N + 2 * H], BF16, tag="w3_raw")
+        w2_g = late_bf16[:, 0 : PACK * N]
+        pairs = [late_bf16[:, PACK * N + a * H : PACK * N + (a + 1) * H] for a in range(2)]
+        deal("scalar", w2_g, w2_raw, 0, P // 2)
+
+        def round_turned(a, src, p0, p1):
+            nc.scalar.activation(
+                out=pairs[a].rearrange("v (u p e) -> v u p e", u=2, e=2)[:, :, p0:p1],
+                in_=src[:, 0 : PACK * (p1 - p0)].rearrange("v (p u e) -> v u p e", u=2, e=2),
+                func=COPY,
+            )
+
+        early_rows = (PACK - 1) * P // PACK
+        for a in range(2):
+            round_turned(a, zt_early[a], 0, early_rows)
+
+        acc = [[bank(7, "acc00"), bank(4, "acc01")], [bank(5, "acc10"), bank(6, "acc11")]]
         for a in range(2):
             for t in range(PACK):
                 mx(acc[a][t // 2][:, block(t % 2)], w3q, block(t), eq, block(a), t % 2 == 0, False)
 
-        w2_g = sb("w2_g", [P, PACK * N], BF16)
-        deal("scalar", w2_g, w2_raw, 0, P // 2)
         deal("scalar", w2_g, w2_raw, P // 2, P)
-        last = sb("prod3", [P, D, V], F32, tag="w3_g")
-        prod.append([last[:, d, :] for d in range(D)])
+        new_products(3)
         for a in range(2):
             for d in range(D):
                 gather(3, d, a, a + 1)
-            add_turned(zt_high[a][:, block(1)], 3, a)
+            add_turned(zt_late[a][:, block(0)], 3, a)
         w2q = operand("w2", N)
         quantize(w2q[0][:], w2q[1][:], w2_g[:])
+        back = [bank(2, "back0"), bank(3, "back1")]
 
         oq = operand("out", V)
         out_rows = out_0.rearrange("(p t) v -> p t v", t=PACK)
         out_words = out_1[0].rearrange("p c r -> p (c r)").bitcast(I32)
-        pairs_high = sb("pairs_high", [P, 2 * V], BF16, tag="w2_raw")
         for a in range(2):
             helper = ("scalar", "vector")[a]
-            round_on(
-                "scalar",
-                pairs_high[:, block(a, V)].rearrange("v (p e) -> v p e", e=2),
-                zt_high[a][:, 0:V].rearrange("v (e p) -> v p e", e=2),
-            )
-            nc.tensor.transpose(back[a][:, block(1)], pairs_high[:].bitcast(F32)[:, block(a)], ident[:])
+            round_turned(a, zt_late[a], early_rows, P)
+            for u in range(2):
+                nc.tensor.transpose(back[a][:, block(u)], pairs[a].bitcast(F32)[:, block(u)], ident[:])
             z_g = sb("z_g%d" % a, [P, PACK * HALF], BF16)
             nc.scalar.copy(
                 out=z_g[:].bitcast(F32).rearrange("p (v u) -> p v u", u=2),
@@ -239,15 +238,15 @@ def tile_picked_zfp_relu_po_kernel(
             for t in range(PACK):
                 mx(acc[a][t // 2][:, block(t % 2)], w2q, block(t), zq, slice(0, HALF), False, t % 2 == 1)
             y = sb("y%d" % a, [P, PACK, HALF], F32)
-            for pair, engine in enumerate(("scalar", helper)):
+            for pair in range(2):
                 relu_on(
-                    engine,
+                    helper,
                     y[:, 2 * pair : 2 * pair + 2, :],
                     acc[a][pair][:, 0:V].rearrange("p (t v) -> p t v", t=2),
                 )
             nc.sync.dma_start(out=out_rows[:, :, block(a)], in_=y[:])
             y_g = sb("y_g%d" % a, [P, PACK * HALF], BF16)
-            interleave("vector", y_g, y)
+            interleave(helper, y_g, y)
             quantize(oq[0][:, block(a)], oq[1][:, block(a)], y_g[:])
             nc.sync.dma_start(out=out_words[:, block(a)], in_=oq[0][:, block(a)].bitcast(I32))
         for q in range(QUADS):

@@ -21,6 +21,7 @@ P = 128
 PACK = 4
 HALF = V // 2
 QUADS = 4
+W2_SPLIT = 64
 
 
 def tile_picked_zfp_relu_po_kernel(
@@ -55,11 +56,11 @@ def tile_picked_zfp_relu_po_kernel(
             else:
                 nc.scalar.activation(out=out, in_=in_, func=RELU)
 
-        def deal(engine, grouped, raw, m0, m1):
+        def deal(engine, grouped, raw, u, m0, m1):
             round_on(
                 engine,
-                grouped[:].rearrange("p (t m j) -> p m j t", t=PACK, j=PACK)[:, m0:m1],
-                raw[:].rearrange("p j (m t) -> p m j t", t=PACK)[:, m0:m1],
+                grouped[:].rearrange("p (u e m j) -> p u m j e", u=2, e=2, j=PACK)[:, u, m0:m1],
+                raw[:].rearrange("p j (m u e) -> p u m j e", u=2, e=2)[:, u, m0:m1],
             )
 
         def interleave(engine, grouped, raw):
@@ -185,14 +186,15 @@ def tile_picked_zfp_relu_po_kernel(
         quantize(eq[0][:], eq[1][:], e_g[:])
 
         w3_g = sb("w3_g", [P, PACK * N], BF16, tag="e_raw")
-        deal("scalar", w3_g, w3_raw, 0, P)
+        for u in range(2):
+            deal("scalar", w3_g, w3_raw, u, 0, P)
         w3q = operand("w3", N)
         quantize(w3q[0][:], w3q[1][:], w3_g[:])
 
         late_bf16 = sb("late_bf16", [P, PACK * N + 2 * H], BF16, tag="w3_raw")
         w2_g = late_bf16[:, 0 : PACK * N]
         pairs = [late_bf16[:, PACK * N + a * H : PACK * N + (a + 1) * H] for a in range(2)]
-        deal("scalar", w2_g, w2_raw, 0, P // 2)
+        deal("scalar", w2_g, w2_raw, 0, 0, P)
 
         def round_turned(a, src, p0, p1):
             nc.scalar.activation(
@@ -210,12 +212,13 @@ def tile_picked_zfp_relu_po_kernel(
             for t in range(PACK):
                 mx(acc[a][t // 2][:, block(t % 2)], w3q, block(t), eq, block(a), t % 2 == 0, False)
 
-        deal("scalar", w2_g, w2_raw, P // 2, P)
+        deal("scalar", w2_g, w2_raw, 1, 0, W2_SPLIT)
         new_products(3)
         for a in range(2):
             for d in range(D):
                 gather(3, d, a, a + 1)
             add_turned(zt_late[a][:, block(0)], 3, a)
+        deal("vector", w2_g, w2_raw, 1, W2_SPLIT, P)
         w2q = operand("w2", N)
         quantize(w2q[0][:], w2q[1][:], w2_g[:])
         back = [bank(2, "back0"), bank(3, "back1")]
@@ -238,15 +241,15 @@ def tile_picked_zfp_relu_po_kernel(
             for t in range(PACK):
                 mx(acc[a][t // 2][:, block(t % 2)], w2q, block(t), zq, slice(0, HALF), False, t % 2 == 1)
             y = sb("y%d" % a, [P, PACK, HALF], F32)
-            for pair in range(2):
+            for pair, engine in enumerate(("scalar", helper)):
                 relu_on(
-                    helper,
+                    engine,
                     y[:, 2 * pair : 2 * pair + 2, :],
                     acc[a][pair][:, 0:V].rearrange("p (t v) -> p t v", t=2),
                 )
             nc.sync.dma_start(out=out_rows[:, :, block(a)], in_=y[:])
             y_g = sb("y_g%d" % a, [P, PACK * HALF], BF16)
-            interleave(helper, y_g, y)
+            interleave("vector", y_g, y)
             quantize(oq[0][:, block(a)], oq[1][:, block(a)], y_g[:])
             nc.sync.dma_start(out=out_words[:, block(a)], in_=oq[0][:, block(a)].bitcast(I32))
         for q in range(QUADS):

@@ -21,7 +21,7 @@ P = 128
 PACK = 4
 HALF = V // 2
 QUADS = 4
-W2_SPLIT = 64
+W2_SPLIT = 56
 
 
 def tile_picked_zfp_relu_po_kernel(
@@ -56,11 +56,11 @@ def tile_picked_zfp_relu_po_kernel(
             else:
                 nc.scalar.activation(out=out, in_=in_, func=RELU)
 
-        def deal(engine, grouped, raw, u, m0, m1):
+        def deal(engine, grouped, raw, m0, m1):
             round_on(
                 engine,
-                grouped[:].rearrange("p (u e m j) -> p u m j e", u=2, e=2, j=PACK)[:, u, m0:m1],
-                raw[:].rearrange("p j (m u e) -> p u m j e", u=2, e=2)[:, u, m0:m1],
+                grouped[:].rearrange("p (t m j) -> p m j t", t=PACK, j=PACK)[:, m0:m1],
+                raw[:].rearrange("p j (m t) -> p m j t", t=PACK)[:, m0:m1],
             )
 
         def interleave(engine, grouped, raw):
@@ -149,7 +149,7 @@ def tile_picked_zfp_relu_po_kernel(
         for t, src in ((1, h1), (2, h2), (3, h3)):
             relu_on("scalar", h[t][:], src[:])
 
-        reuse = ("xw_all", None, None, "e_raw")
+        reuse = ("xw_all", None, None, None)
         prod = []
 
         def new_products(t):
@@ -186,15 +186,12 @@ def tile_picked_zfp_relu_po_kernel(
         quantize(eq[0][:], eq[1][:], e_g[:])
 
         w3_g = sb("w3_g", [P, PACK * N], BF16, tag="e_raw")
-        for u in range(2):
-            deal("scalar", w3_g, w3_raw, u, 0, P)
-        w3q = operand("w3", N)
-        quantize(w3q[0][:], w3q[1][:], w3_g[:])
+        deal("scalar", w3_g, w3_raw, 0, P)
 
         late_bf16 = sb("late_bf16", [P, PACK * N + 2 * H], BF16, tag="w3_raw")
         w2_g = late_bf16[:, 0 : PACK * N]
         pairs = [late_bf16[:, PACK * N + a * H : PACK * N + (a + 1) * H] for a in range(2)]
-        deal("scalar", w2_g, w2_raw, 0, 0, P)
+        deal("scalar", w2_g, w2_raw, 0, W2_SPLIT)
 
         def round_turned(a, src, p0, p1):
             nc.scalar.activation(
@@ -207,18 +204,14 @@ def tile_picked_zfp_relu_po_kernel(
         for a in range(2):
             round_turned(a, zt_early[a], 0, early_rows)
 
-        acc = [[bank(7, "acc00"), bank(4, "acc01")], [bank(5, "acc10"), bank(6, "acc11")]]
-        for a in range(2):
-            for t in range(PACK):
-                mx(acc[a][t // 2][:, block(t % 2)], w3q, block(t), eq, block(a), t % 2 == 0, False)
-
-        deal("scalar", w2_g, w2_raw, 1, 0, W2_SPLIT)
         new_products(3)
         for a in range(2):
             for d in range(D):
                 gather(3, d, a, a + 1)
             add_turned(zt_late[a][:, block(0)], 3, a)
-        deal("vector", w2_g, w2_raw, 1, W2_SPLIT, P)
+        w3q = operand("w3", N)
+        quantize(w3q[0][:], w3q[1][:], w3_g[:])
+        deal("vector", w2_g, w2_raw, W2_SPLIT, P)
         w2q = operand("w2", N)
         quantize(w2q[0][:], w2q[1][:], w2_g[:])
         back = [bank(2, "back0"), bank(3, "back1")]
@@ -226,8 +219,8 @@ def tile_picked_zfp_relu_po_kernel(
         oq = operand("out", V)
         out_rows = out_0.rearrange("(p t) v -> p t v", t=PACK)
         out_words = out_1[0].rearrange("p c r -> p (c r)").bitcast(I32)
+        zq = []
         for a in range(2):
-            helper = ("scalar", "vector")[a]
             round_turned(a, zt_late[a], early_rows, P)
             for u in range(2):
                 nc.tensor.transpose(back[a][:, block(u)], pairs[a].bitcast(F32)[:, block(u)], ident[:])
@@ -236,10 +229,17 @@ def tile_picked_zfp_relu_po_kernel(
                 out=z_g[:].bitcast(F32).rearrange("p (v u) -> p v u", u=2),
                 in_=back[a][:, 0:V].rearrange("p (u v) -> p v u", u=2),
             )
-            zq = operand("z%d" % a, HALF)
-            quantize(zq[0][:], zq[1][:], z_g[:])
+            zq.append(operand("z%d" % a, HALF))
+            quantize(zq[a][0][:], zq[a][1][:], z_g[:])
+
+        acc = [[bank(1, "acc00"), bank(0, "acc01")], [bank(2, "acc10"), bank(3, "acc11")]]
+        for a in range(2):
             for t in range(PACK):
-                mx(acc[a][t // 2][:, block(t % 2)], w2q, block(t), zq, slice(0, HALF), False, t % 2 == 1)
+                mx(acc[a][t // 2][:, block(t % 2)], w3q, block(t), eq, block(a), t % 2 == 0, False)
+        for a in range(2):
+            helper = ("scalar", "vector")[a]
+            for t in range(PACK):
+                mx(acc[a][t // 2][:, block(t % 2)], w2q, block(t), zq[a], slice(0, HALF), False, t % 2 == 1)
             y = sb("y%d" % a, [P, PACK, HALF], F32)
             for pair, engine in enumerate(("scalar", helper)):
                 relu_on(

@@ -21,6 +21,8 @@ P = 128
 PACK = 4
 HALF = V // 2
 QUADS = 4
+LIST_ROWS = 16
+BANK_COLS = 512
 W2_SPLIT = 56
 
 
@@ -37,7 +39,10 @@ def tile_picked_zfp_relu_po_kernel(
             return keep.tile(shape, dtype, name=name, tag=tag or name, align_bytes=64)
 
         def bank(number, name):
-            return psum.tile([P, 512], F32, name=name, tag="bank%d" % number)
+            return psum.tile([P, BANK_COLS], F32, name=name, tag="bank%d" % number)
+
+        def block(i, width=P):
+            return slice(i * width, (i + 1) * width)
 
         def load_rows(name, src, cols):
             raw = sb(name, [P, PACK, cols.stop - cols.start], F32)
@@ -56,13 +61,6 @@ def tile_picked_zfp_relu_po_kernel(
             else:
                 nc.scalar.activation(out=out, in_=in_, func=RELU)
 
-        def deal(engine, grouped, raw, m0, m1):
-            round_on(
-                engine,
-                grouped[:].rearrange("p (t m j) -> p m j t", t=PACK, j=PACK)[:, m0:m1],
-                raw[:].rearrange("p j (m t) -> p m j t", t=PACK)[:, m0:m1],
-            )
-
         def interleave(engine, grouped, raw):
             round_on(
                 engine,
@@ -70,27 +68,31 @@ def tile_picked_zfp_relu_po_kernel(
                 raw[:].rearrange("p j (c i) -> p c j i", i=4),
             )
 
-        def quantize(codes, scales, grouped):
-            nc.vector.quantize_mx(out=codes.bitcast(FP8X4), scales=scales, in_=grouped)
-
-        def mx(out, a, cols_a, b, cols_b, start, stop):
-            nc.tensor.matmul_mx(
-                out=out,
-                lhsT=a[0][:, cols_a].bitcast(FP8X4),
-                lhsT_scale=a[1][:, cols_a],
-                rhs=b[0][:, cols_b].bitcast(FP8X4),
-                rhs_scale=b[1][:, cols_b],
-                start=start,
-                stop=stop,
+        def deal(engine, grouped, raw, m0, m1):
+            round_on(
+                engine,
+                grouped[:].rearrange("p (t m j) -> p m j t", t=PACK, j=PACK)[:, m0:m1],
+                raw[:].rearrange("p j (m t) -> p m j t", t=PACK)[:, m0:m1],
             )
 
         def operand(name, width):
             return sb(name + "_codes", [P, width], U32), sb(name + "_scales", [P, width], U8)
 
-        def block(i, width=P):
-            return slice(i * width, (i + 1) * width)
+        def quantize(codes, scales, grouped):
+            nc.vector.quantize_mx(out=codes.bitcast(FP8X4), scales=scales, in_=grouped)
 
-        offs_sb = lists.tile([P, S // 16], U16, name="offs_sb")
+        def mx(out, lhs, lhs_cols, rhs, rhs_cols, start, stop):
+            nc.tensor.matmul_mx(
+                out=out,
+                lhsT=lhs[0][:, lhs_cols].bitcast(FP8X4),
+                lhsT_scale=lhs[1][:, lhs_cols],
+                rhs=rhs[0][:, rhs_cols].bitcast(FP8X4),
+                rhs_scale=rhs[1][:, rhs_cols],
+                start=start,
+                stop=stop,
+            )
+
+        offs_sb = lists.tile([P, S // LIST_ROWS], U16, name="offs_sb")
         nc.sync.dma_start(offs_sb[:], offs)
         w1_raw = [load_rows("w1_raw0", w1, block(0, H // 2))]
 
@@ -107,13 +109,13 @@ def tile_picked_zfp_relu_po_kernel(
         w1_raw.append(load_rows("w1_raw1", w1, block(1, H // 2)))
         pos_sb = []
         for d, pos in enumerate((pos1, pos2, pos3)):
-            one = lists.tile([P, V // 16], U16, name="pos%d_sb" % d)
+            one = lists.tile([P, V // LIST_ROWS], U16, name="pos%d_sb" % d)
             nc.sync.dma_start(one[:], pos)
             pos_sb.append(one)
         gate_sb = sb("gate_sb", [P, D, V], F32)
         nc.sync.dma_start(out=gate_sb[:], in_=gate.rearrange("d p v -> p d v"))
-        e_raw = load_rows("e_raw", eT, slice(0, V))
         w3_raw = load_rows("w3_raw", w3, slice(0, N))
+        e_raw = load_rows("e_raw", eT, slice(0, V))
         w2_raw = load_rows("w2_raw", w2, slice(0, N))
 
         ident = sb("ident", [P, P], F32)
@@ -127,40 +129,38 @@ def tile_picked_zfp_relu_po_kernel(
         interleave("scalar", w1_g[0], w1_raw[0])
         quantize(w1q[0][0][:], w1q[0][1][:], w1_g[0][:])
 
-        for a in range(2):
+        first, second, whole = block(0, S // 2), block(1, S // 2), slice(0, S)
+        for i in range(2):
             nc.vector.tensor_copy(
-                out=xq[0][:, block(a, S // 2)],
-                in_=xw_all[:].bitcast(U32).indirect(offs_sb[:, block(a, S // 32)]),
+                out=xq[0][:, block(i, S // 2)],
+                in_=xw_all[:].bitcast(U32).indirect(offs_sb[:, block(i, S // 2 // LIST_ROWS)]),
             )
         interleave("vector", w1_g[1], w1_raw[1])
         quantize(w1q[1][0][:], w1q[1][1][:], w1_g[1][:])
 
         h = [sb("h%d" % t, [P, S], F32) for t in range(PACK)]
-        h0a, h0b, h1, h2, h3 = [bank(i, "hbank%d" % i) for i in range(5)]
-        first, second = block(0, S // 2), block(1, S // 2)
-        mx(h0a[:, first], w1q[0], block(0), xq, first, True, True)
-        mx(h1[:, first], w1q[0], block(1), xq, first, True, True)
-        mx(h0b[:, first], w1q[0], block(0), xq, second, True, True)
-        mx(h1[:, second], w1q[0], block(1), xq, second, True, True)
-        mx(h2[:], w1q[1], block(0), xq, slice(0, S), True, True)
-        mx(h3[:], w1q[1], block(1), xq, slice(0, S), True, True)
-        relu_on("scalar", h[0][:, first], h0a[:, first])
-        relu_on("scalar", h[0][:, second], h0b[:, first])
-        for t, src in ((1, h1), (2, h2), (3, h3)):
+        h0_first, h0_second, h1_bank, h2_bank, h3_bank = [bank(i, "hbank%d" % i) for i in range(PACK + 1)]
+        mx(h0_first[:, first], w1q[0], block(0), xq, first, True, True)
+        mx(h1_bank[:, first], w1q[0], block(1), xq, first, True, True)
+        mx(h0_second[:, first], w1q[0], block(0), xq, second, True, True)
+        mx(h1_bank[:, second], w1q[0], block(1), xq, second, True, True)
+        mx(h2_bank[:], w1q[1], block(0), xq, whole, True, True)
+        mx(h3_bank[:], w1q[1], block(1), xq, whole, True, True)
+        relu_on("scalar", h[0][:, first], h0_first[:, first])
+        relu_on("scalar", h[0][:, second], h0_second[:, first])
+        for t, src in ((1, h1_bank), (2, h2_bank), (3, h3_bank)):
             relu_on("scalar", h[t][:], src[:])
 
-        reuse = ("xw_all", None, None, None)
         prod = []
 
         def new_products(t):
-            three = sb("prod%d" % t, [P, D, V], F32, tag=reuse[t])
-            prod.append([three[:, d, :] for d in range(D)])
+            prod.append(sb("prod%d" % t, [P, D, V], F32, tag="xw_all" if t == 0 else None))
 
         def gather(t, d, a0, a1):
             cols = slice(a0 * HALF, a1 * HALF)
             nc.vector.tensor_tensor(
-                out=prod[t][d][:, cols],
-                in0=h[t][:].indirect(pos_sb[d][:, a0 * HALF // 16 : a1 * HALF // 16]),
+                out=prod[t][:, d, cols],
+                in0=h[t][:].indirect(pos_sb[d][:, a0 * HALF // LIST_ROWS : a1 * HALF // LIST_ROWS]),
                 in1=gate_sb[:, d, cols],
                 op=MULT,
             )
@@ -168,30 +168,27 @@ def tile_picked_zfp_relu_po_kernel(
         def add_turned(out, t, a):
             for d in range(D):
                 nc.tensor.matmul(
-                    out, lhsT=prod[t][d][:, block(a)], rhs=ident[:], is_transpose=True, start=(d == 0), stop=(d == D - 1)
+                    out, lhsT=prod[t][:, d, block(a)], rhs=ident[:], is_transpose=True, start=(d == 0), stop=(d == D - 1)
                 )
 
+        last = PACK - 1
         zt_early = [bank(5, "zt_early0"), bank(6, "zt_early1")]
         zt_late = [bank(0, "zt_late0"), bank(1, "zt_late1")]
-        for t in range(PACK - 1):
+        for t in range(last):
             new_products(t)
             for d in range(D):
                 gather(t, d, 0, 2)
             for a in range(2):
                 add_turned(zt_early[a][:, block(t)], t, a)
 
-        e_g = sb("e_g", [P, PACK * V], BF16, tag="w1_1_codes")
-        interleave("scalar", e_g, e_raw)
-        eq = operand("e", V)
-        quantize(eq[0][:], eq[1][:], e_g[:])
-
-        w3_g = sb("w3_g", [P, PACK * N], BF16, tag="e_raw")
+        w3_g = sb("w3_g", [P, PACK * N], BF16, tag="w1_1_codes")
         deal("scalar", w3_g, w3_raw, 0, P)
 
-        late_bf16 = sb("late_bf16", [P, PACK * N + 2 * H], BF16, tag="w3_raw")
-        w2_g = late_bf16[:, 0 : PACK * N]
-        pairs = [late_bf16[:, PACK * N + a * H : PACK * N + (a + 1) * H] for a in range(2)]
-        deal("scalar", w2_g, w2_raw, 0, W2_SPLIT)
+        after_w3 = sb("after_w3", [P, PACK * N + 2 * H + PACK * V], BF16, tag="w3_raw")
+        w2_g = after_w3[:, 0 : PACK * N]
+        pairs = [after_w3[:, PACK * N + a * H : PACK * N + (a + 1) * H] for a in range(2)]
+        e_g = after_w3[:, PACK * N + 2 * H :]
+        interleave("scalar", e_g, e_raw)
 
         def round_turned(a, src, p0, p1):
             nc.scalar.activation(
@@ -200,17 +197,21 @@ def tile_picked_zfp_relu_po_kernel(
                 func=COPY,
             )
 
-        early_rows = (PACK - 1) * P // PACK
+        early_p = last * P // PACK
         for a in range(2):
-            round_turned(a, zt_early[a], 0, early_rows)
+            round_turned(a, zt_early[a], 0, early_p)
+        deal("scalar", w2_g, w2_raw, 0, W2_SPLIT)
 
-        new_products(3)
+        new_products(last)
         for a in range(2):
             for d in range(D):
-                gather(3, d, a, a + 1)
-            add_turned(zt_late[a][:, block(0)], 3, a)
+                gather(last, d, a, a + 1)
+            add_turned(zt_late[a][:, block(0)], last, a)
+
         w3q = operand("w3", N)
         quantize(w3q[0][:], w3q[1][:], w3_g[:])
+        eq = operand("e", V)
+        quantize(eq[0][:], eq[1][:], e_g[:])
         deal("vector", w2_g, w2_raw, W2_SPLIT, P)
         w2q = operand("w2", N)
         quantize(w2q[0][:], w2q[1][:], w2_g[:])
@@ -221,13 +222,13 @@ def tile_picked_zfp_relu_po_kernel(
         out_words = out_1[0].rearrange("p c r -> p (c r)").bitcast(I32)
         zq = []
         for a in range(2):
-            round_turned(a, zt_late[a], early_rows, P)
+            round_turned(a, zt_late[a], early_p, P)
             for u in range(2):
                 nc.tensor.transpose(back[a][:, block(u)], pairs[a].bitcast(F32)[:, block(u)], ident[:])
             z_g = sb("z_g%d" % a, [P, PACK * HALF], BF16)
             nc.scalar.copy(
                 out=z_g[:].bitcast(F32).rearrange("p (v u) -> p v u", u=2),
-                in_=back[a][:, 0:V].rearrange("p (u v) -> p v u", u=2),
+                in_=back[a][:, 0 : 2 * HALF].rearrange("p (u v) -> p v u", u=2),
             )
             zq.append(operand("z%d" % a, HALF))
             quantize(zq[a][0][:], zq[a][1][:], z_g[:])
@@ -237,21 +238,21 @@ def tile_picked_zfp_relu_po_kernel(
             for t in range(PACK):
                 mx(acc[a][t // 2][:, block(t % 2)], w3q, block(t), eq, block(a), t % 2 == 0, False)
         for a in range(2):
-            helper = ("scalar", "vector")[a]
             for t in range(PACK):
                 mx(acc[a][t // 2][:, block(t % 2)], w2q, block(t), zq[a], slice(0, HALF), False, t % 2 == 1)
             y = sb("y%d" % a, [P, PACK, HALF], F32)
-            for pair, engine in enumerate(("scalar", helper)):
+            for r, engine in enumerate(("scalar", "vector" if a == 1 else "scalar")):
                 relu_on(
                     engine,
-                    y[:, 2 * pair : 2 * pair + 2, :],
-                    acc[a][pair][:, 0:V].rearrange("p (t v) -> p t v", t=2),
+                    y[:, 2 * r : 2 * r + 2, :],
+                    acc[a][r][:, 0 : 2 * HALF].rearrange("p (t v) -> p t v", t=2),
                 )
             nc.sync.dma_start(out=out_rows[:, :, block(a)], in_=y[:])
             y_g = sb("y_g%d" % a, [P, PACK * HALF], BF16)
             interleave("vector", y_g, y)
             quantize(oq[0][:, block(a)], oq[1][:, block(a)], y_g[:])
             nc.sync.dma_start(out=out_words[:, block(a)], in_=oq[0][:, block(a)].bitcast(I32))
+
         for q in range(QUADS):
             queue = nc.scalar if q % 2 else nc.sync
             queue.dma_start(

from contextlib import ExitStack

import concourse.mybir as mybir
from concourse.masks import make_identity

K, T, S, D, V, H, N = 512, 2048, 512, 3, 256, 512, 512
FLOPS = 2 * (K * H * S + H * N * V + K * N * V)

F32 = mybir.dt.float32
BF16 = mybir.dt.bfloat16
I32 = mybir.dt.int32
U32 = mybir.dt.uint32
U16 = mybir.dt.uint16
U8 = mybir.dt.uint8
FP8X4 = mybir.dt.float8_e4m3fn_x4
MULT = mybir.AluOpType.mult
COPY = mybir.ActivationFunctionType.Copy
RELU = mybir.ActivationFunctionType.Relu

P = 128
PACK = 4
HALF = V // 2
QUADS = 4
LIST_ROWS = 16
BANK_COLS = 512
W2_SPLIT = 56


def tile_picked_zfp_relu_po_kernel(
    tc, x_words, x_scales, w1, w2, gate, eT, w3, offs, pos1, pos2, pos3, out_0, out_1, out_2
):
    nc = tc.nc
    with ExitStack() as ctx:
        lists = ctx.enter_context(tc.tile_pool(name="lists", bufs=1))
        keep = ctx.enter_context(tc.tile_pool(name="keep", bufs=1))
        psum = ctx.enter_context(tc.psum_pool(name="psum", bufs=1))

        def sb(name, shape, dtype, tag=None):
            return keep.tile(shape, dtype, name=name, tag=tag or name, align_bytes=64)

        def bank(number, name):
            return psum.tile([P, BANK_COLS], F32, name=name, tag="bank%d" % number)

        def block(i, width=P):
            return slice(i * width, (i + 1) * width)

        def load_rows(name, src, cols):
            raw = sb(name, [P, PACK, cols.stop - cols.start], F32)
            nc.sync.dma_start(out=raw[:], in_=src.rearrange("(p j) c -> p j c", j=PACK)[:, :, cols])
            return raw

        def round_on(engine, out, in_):
            if engine == "vector":
                nc.vector.tensor_copy(out=out, in_=in_)
            else:
                nc.scalar.activation(out=out, in_=in_, func=COPY)

        def relu_on(engine, out, in_):
            if engine == "vector":
                nc.vector.tensor_scalar_max(out=out, in0=in_, scalar1=0.0)
            else:
                nc.scalar.activation(out=out, in_=in_, func=RELU)

        def interleave(engine, grouped, raw):
            round_on(
                engine,
                grouped[:].rearrange("p (c i j) -> p c j i", i=4, j=PACK),
                raw[:].rearrange("p j (c i) -> p c j i", i=4),
            )

        def deal(engine, grouped, raw, m0, m1):
            round_on(
                engine,
                grouped[:].rearrange("p (t m j) -> p m j t", t=PACK, j=PACK)[:, m0:m1],
                raw[:].rearrange("p j (m t) -> p m j t", t=PACK)[:, m0:m1],
            )

        def operand(name, width):
            return sb(name + "_codes", [P, width], U32), sb(name + "_scales", [P, width], U8)

        def quantize(codes, scales, grouped):
            nc.vector.quantize_mx(out=codes.bitcast(FP8X4), scales=scales, in_=grouped)

        def mx(out, lhs, lhs_cols, rhs, rhs_cols, start, stop):
            nc.tensor.matmul_mx(
                out=out,
                lhsT=lhs[0][:, lhs_cols].bitcast(FP8X4),
                lhsT_scale=lhs[1][:, lhs_cols],
                rhs=rhs[0][:, rhs_cols].bitcast(FP8X4),
                rhs_scale=rhs[1][:, rhs_cols],
                start=start,
                stop=stop,
            )

        offs_sb = lists.tile([P, S // LIST_ROWS], U16, name="offs_sb")
        nc.sync.dma_start(offs_sb[:], offs)
        w1_raw = [load_rows("w1_raw0", w1, block(0, H // 2))]

        xs_all = sb("xs_all", [P, T], U8)
        nc.gpsimd.memset(xs_all[:].bitcast(I32), 0)
        for q in range(QUADS):
            nc.sync.dma_start(
                out=xs_all[32 * q : 32 * q + 4, :].bitcast(I32),
                in_=x_scales[0, 4 * q : 4 * q + 4, :].bitcast(I32),
            )
        xw_all = sb("xw_all", [P, T], I32)
        nc.sync.dma_start(out=xw_all[:], in_=x_words[0].rearrange("p c r -> p (c r)").bitcast(I32))

        w1_raw.append(load_rows("w1_raw1", w1, block(1, H // 2)))
        pos_sb = []
        for d, pos in enumerate((pos1, pos2, pos3)):
            one = lists.tile([P, V // LIST_ROWS], U16, name="pos%d_sb" % d)
            nc.sync.dma_start(one[:], pos)
            pos_sb.append(one)
        gate_sb = sb("gate_sb", [P, D, V], F32)
        nc.sync.dma_start(out=gate_sb[:], in_=gate.rearrange("d p v -> p d v"))
        w3_raw = load_rows("w3_raw", w3, slice(0, N))
        e_raw = load_rows("e_raw", eT, slice(0, V))
        w2_raw = load_rows("w2_raw", w2, slice(0, N))

        ident = sb("ident", [P, P], F32)
        make_identity(nc, ident[:])

        xq = operand("x", S)
        nc.vector.tensor_copy(out=xq[1][:], in_=xs_all[:].indirect(offs_sb[:]))

        w1_g = [sb("w1_g0", [P, PACK * H // 2], BF16), sb("w1_g1", [P, PACK * H // 2], BF16, tag="xw_all")]
        w1q = [operand("w1_%d" % i, H // 2) for i in range(2)]
        interleave("scalar", w1_g[0], w1_raw[0])
        quantize(w1q[0][0][:], w1q[0][1][:], w1_g[0][:])

        first, second, whole = block(0, S // 2), block(1, S // 2), slice(0, S)
        for i in range(2):
            nc.vector.tensor_copy(
                out=xq[0][:, block(i, S // 2)],
                in_=xw_all[:].bitcast(U32).indirect(offs_sb[:, block(i, S // 2 // LIST_ROWS)]),
            )
        interleave("vector", w1_g[1], w1_raw[1])
        quantize(w1q[1][0][:], w1q[1][1][:], w1_g[1][:])

        h = [sb("h%d" % t, [P, S], F32) for t in range(PACK)]
        h0_first, h0_second, h1_bank, h2_bank, h3_bank = [bank(i, "hbank%d" % i) for i in range(PACK + 1)]
        mx(h0_first[:, first], w1q[0], block(0), xq, first, True, True)
        mx(h1_bank[:, first], w1q[0], block(1), xq, first, True, True)
        mx(h0_second[:, first], w1q[0], block(0), xq, second, True, True)
        mx(h1_bank[:, second], w1q[0], block(1), xq, second, True, True)
        mx(h2_bank[:], w1q[1], block(0), xq, whole, True, True)
        mx(h3_bank[:], w1q[1], block(1), xq, whole, True, True)
        relu_on("scalar", h[0][:, first], h0_first[:, first])
        relu_on("scalar", h[0][:, second], h0_second[:, first])
        for t, src in ((1, h1_bank), (2, h2_bank), (3, h3_bank)):
            relu_on("scalar", h[t][:], src[:])

        prod = []

        def new_products(t):
            prod.append(sb("prod%d" % t, [P, D, V], F32, tag="xw_all" if t == 0 else None))

        def gather(t, d, a0, a1):
            cols = slice(a0 * HALF, a1 * HALF)
            nc.vector.tensor_tensor(
                out=prod[t][:, d, cols],
                in0=h[t][:].indirect(pos_sb[d][:, a0 * HALF // LIST_ROWS : a1 * HALF // LIST_ROWS]),
                in1=gate_sb[:, d, cols],
                op=MULT,
            )

        def add_turned(out, t, a):
            for d in range(D):
                nc.tensor.matmul(
                    out, lhsT=prod[t][:, d, block(a)], rhs=ident[:], is_transpose=True, start=(d == 0), stop=(d == D - 1)
                )

        last = PACK - 1
        zt_early = [bank(5, "zt_early0"), bank(6, "zt_early1")]
        zt_late = [bank(0, "zt_late0"), bank(1, "zt_late1")]
        for t in range(last):
            new_products(t)
            for d in range(D):
                gather(t, d, 0, 2)
            for a in range(2):
                add_turned(zt_early[a][:, block(t)], t, a)

        w3_g = sb("w3_g", [P, PACK * N], BF16, tag="w1_1_codes")
        deal("scalar", w3_g, w3_raw, 0, P)

        after_w3 = sb("after_w3", [P, PACK * N + 2 * H + PACK * V], BF16, tag="w3_raw")
        w2_g = after_w3[:, 0 : PACK * N]
        pairs = [after_w3[:, PACK * N + a * H : PACK * N + (a + 1) * H] for a in range(2)]
        e_g = after_w3[:, PACK * N + 2 * H :]
        interleave("scalar", e_g, e_raw)

        def round_turned(a, src, p0, p1):
            nc.scalar.activation(
                out=pairs[a].rearrange("v (u p e) -> v u p e", u=2, e=2)[:, :, p0:p1],
                in_=src[:, 0 : PACK * (p1 - p0)].rearrange("v (p u e) -> v u p e", u=2, e=2),
                func=COPY,
            )

        early_p = last * P // PACK
        for a in range(2):
            round_turned(a, zt_early[a], 0, early_p)
        deal("scalar", w2_g, w2_raw, 0, W2_SPLIT)

        new_products(last)
        for a in range(2):
            for d in range(D):
                gather(last, d, a, a + 1)
            add_turned(zt_late[a][:, block(0)], last, a)

        w3q = operand("w3", N)
        quantize(w3q[0][:], w3q[1][:], w3_g[:])
        eq = operand("e", V)
        quantize(eq[0][:], eq[1][:], e_g[:])
        deal("vector", w2_g, w2_raw, W2_SPLIT, P)
        w2q = operand("w2", N)
        quantize(w2q[0][:], w2q[1][:], w2_g[:])
        back = [bank(2, "back0"), bank(3, "back1")]

        oq = operand("out", V)
        out_rows = out_0.rearrange("(p t) v -> p t v", t=PACK)
        out_words = out_1[0].rearrange("p c r -> p (c r)").bitcast(I32)
        zq = []
        for a in range(2):
            round_turned(a, zt_late[a], early_p, P)
            for u in range(2):
                nc.tensor.transpose(back[a][:, block(u)], pairs[a].bitcast(F32)[:, block(u)], ident[:])
            z_g = sb("z_g%d" % a, [P, PACK * HALF], BF16)
            nc.scalar.copy(
                out=z_g[:].bitcast(F32).rearrange("p (v u) -> p v u", u=2),
                in_=back[a][:, 0 : 2 * HALF].rearrange("p (u v) -> p v u", u=2),
            )
            zq.append(operand("z%d" % a, HALF))
            quantize(zq[a][0][:], zq[a][1][:], z_g[:])

        acc = [[bank(1, "acc00"), bank(0, "acc01")], [bank(2, "acc10"), bank(3, "acc11")]]
        for a in range(2):
            for t in range(PACK):
                mx(acc[a][t // 2][:, block(t % 2)], w3q, block(t), eq, block(a), t % 2 == 0, False)
        for a in range(2):
            for t in range(PACK):
                mx(acc[a][t // 2][:, block(t % 2)], w2q, block(t), zq[a], slice(0, HALF), False, t % 2 == 1)
            y = sb("y%d" % a, [P, PACK, HALF], F32)
            for r, engine in enumerate(("scalar", "vector" if a == 1 else "scalar")):
                relu_on(
                    engine,
                    y[:, 2 * r : 2 * r + 2, :],
                    acc[a][r][:, 0 : 2 * HALF].rearrange("p (t v) -> p t v", t=2),
                )
            nc.sync.dma_start(out=out_rows[:, :, block(a)], in_=y[:])
            y_g = sb("y_g%d" % a, [P, PACK * HALF], BF16)
            interleave("vector", y_g, y)
            quantize(oq[0][:, block(a)], oq[1][:, block(a)], y_g[:])
            nc.sync.dma_start(out=out_words[:, block(a)], in_=oq[0][:, block(a)].bitcast(I32))

        for q in range(QUADS):
            queue = nc.scalar if q % 2 else nc.sync
            queue.dma_start(
                out=out_2[0, 4 * q : 4 * q + 4, :].bitcast(I32),
                in_=oq[1][32 * q : 32 * q + 4, :].bitcast(I32),
            )
